import numpy as np
import ml_dtypes


def mxq(x, axis, fmt="e4m3"):
    dtype, down = {"e4m3": (ml_dtypes.float8_e4m3fn, 7), "e5m2": (ml_dtypes.float8_e5m2, 14)}[fmt]
    v = np.moveaxis(np.asarray(x, np.float32).astype(ml_dtypes.bfloat16).astype(np.float64), axis, -1)
    blocks = v.reshape(v.shape[:-1] + (-1, 32))
    amax = np.abs(blocks).max(-1, keepdims=True)
    byte = np.maximum(np.where(amax > 0, np.frexp(amax)[1] - 1 + 127, 0) - down, 1)
    scale = np.exp2(byte - 127.0)
    codes = (blocks / scale).astype(np.float32).astype(dtype).astype(np.float64)
    return np.moveaxis((codes * scale).reshape(v.shape), -1, axis)


WIDE = False


def mx_kscale(k):
    if not WIDE:
        return np.ones(k)
    levels = np.array([10, -10, 5, -5, 0])
    if k % 512:
        return np.exp2(np.random.permutation(np.resize(levels, k // 32))).repeat(32)
    a = np.empty((k // 512, 16))
    for p in range(k // 512):
        a[p, :8] = np.random.permutation(np.resize(levels, 8))
        for g in range(8):
            far = levels[np.abs(levels - a[p, g]) >= 10]
            a[p, g + 8] = far[np.random.randint(len(far))]
    return np.exp2(a.ravel()).repeat(32)


BF16 = ml_dtypes.bfloat16


def bf(x):
    return np.asarray(x, np.float32).astype(BF16)


def f64(x):
    return np.asarray(x).astype(np.float64)


E2M1 = np.array([0.0, 0.5, 1.0, 1.5, 2.0, 3.0, 4.0, 6.0, -0.0, -0.5, -1.0, -1.5, -2.0, -3.0, -4.0, -6.0])


def pack_weight(w, fmt):
    k, n = w.shape
    w = f64(bf(w)).reshape(k // 32, 32, n)
    amax = np.abs(w).max(1)
    if fmt == "e4m3":
        byte = np.frexp(amax)[1] - 1 + 127 - 7
    else:
        mant, ex = np.frexp(amax / 6.0)
        byte = np.where(mant > 0.5, ex, ex - 1) + 127
    byte = np.clip(np.where(amax > 0, byte, 1), 1, 254)
    scaled = (w * np.exp2(127.0 - byte)[:, None, :]).reshape(k, n).astype(np.float32)
    by_word = np.ascontiguousarray(scaled.reshape(k // 512, 128, 4, n).transpose(0, 1, 3, 2))
    if fmt == "e4m3":
        words = by_word.astype(ml_dtypes.float8_e4m3fn).view(np.uint8)
    else:
        c = by_word.astype(ml_dtypes.float4_e2m1fn).view(np.uint8) & 0xF
        words = c[..., 0::2] | (c[..., 1::2] << 4)
    return np.ascontiguousarray(words), np.ascontiguousarray(byte.astype(np.uint8).reshape(k // 512, 16, n))


def unpack_weight(words, scales, fmt):
    g, p, n, _ = words.shape
    if fmt == "e4m3":
        vals = np.ascontiguousarray(words).view(ml_dtypes.float8_e4m3fn).astype(np.float64)
    else:
        nib = np.empty((g, p, n, 4), np.uint8)
        nib[..., 0::2] = words & 0xF
        nib[..., 1::2] = words >> 4
        vals = E2M1[nib]
    vals = vals * np.repeat(np.exp2(scales.astype(np.float64) - 127.0), 8, axis=1)[..., None]
    return vals.transpose(0, 1, 3, 2).reshape(g * 512, n)
def pack4(w):
    words, scales = pack_weight(w, "e2m1")
    return words.reshape(words.shape[0], 128, -1), scales


def unpack4(words, scales):
    return unpack_weight(words.reshape(words.shape[0], 128, -1, 2), scales, "e2m1")


M, V, D = 1024, 1024, 1536


def setup_inputs():
    s, t = mx_kscale(V), mx_kscale(D)
    v1 = np.random.standard_normal((M, V)) * s
    x = np.random.standard_normal((M, D)) * t
    wo = np.random.standard_normal((V, D)) / np.sqrt(V) / s[:, None]
    wf = np.random.standard_normal((D, D)) / np.sqrt(D) / t[:, None]
    wf_words, wf_scales = pack4(wf)
    return {"v1": bf(v1),
            "x": bf(x),
            "mix": bf(np.random.standard_normal((M, 1))),
            "wo": bf(wo),
            "wf_words": wf_words,
            "wf_scales": wf_scales,
            "bias": bf(0.3 * np.random.standard_normal(D))}


def reference(v1, x, mix, wo, wf_words, wf_scales, bias):
    lam = 1.0 / (1.0 + np.exp(-f64(mix)))
    old = lam * f64(v1)
    new = (1.0 - lam) * f64(x)
    y = ((mxq(old, 1, "e4m3") @ mxq(f64(wo), 0, "e4m3"))
         + (mxq(new, 1, "e4m3") @ unpack4(wf_words, wf_scales)))
    return y + f64(bias)

@@ -1,0 +1,319 @@
+from contextlib import ExitStack
+
+import concourse.mybir as mybir
+from concourse.masks import make_identity
+
+M, V, D = 1024, 1024, 1536
+FLOPS = 2 * M * (V + D) * D
+
+F32 = mybir.dt.float32
+BF16 = mybir.dt.bfloat16
+I32 = mybir.dt.int32
+U32 = mybir.dt.uint32
+U8 = mybir.dt.uint8
+FP8X4 = mybir.dt.float8_e4m3fn_x4
+FP4X4 = mybir.dt.float4_e2m1fn_x4
+ACT = mybir.ActivationFunctionType
+ALU = mybir.AluOpType
+ENG = mybir.EngineType
+
+P = 128
+TILES = M // P
+NC = 512
+CHUNKS = D // NC
+X_PASSES = D // 512
+V_PASSES = V // 512
+
+
+def tile_value_residual_projection_s1_kernel(tc, v1, x, mix, wo, wf_words, wf_scales, bias, out):
+    nc = tc.nc
+    x_rows = x.rearrange("(p i) k -> p i k", i=TILES)
+    v_rows = v1.rearrange("(p i) k -> p i k", i=TILES)
+    out_rows = out.rearrange("(p i) n -> p i n", i=TILES)
+
+    with ExitStack() as ctx:
+        keep = ctx.enter_context(tc.tile_pool(name="keep", bufs=1))
+        work = ctx.enter_context(tc.tile_pool(name="work", bufs=3))
+        psum = ctx.enter_context(tc.psum_pool(name="psum", bufs=1))
+        ctx.enter_context(tc.manual_schedule(engines={ENG.PE, ENG.SP}))
+
+        free_banks = list(range(8))
+        raw = {}
+        ordered = {}
+        turned = {}
+        grouped = {}
+        codes = {}
+        w_words = {}
+        w_planes = {}
+        wo_raw = {}
+        wo_grouped = {}
+        wo_codes = {}
+        acc = {}
+        res = {}
+
+        def take_bank():
+            b = free_banks.pop(0)
+            bank = psum.tile([P, 512], F32, tag="bank%d" % b, name="bank%d" % b)
+            return b, bank
+
+        def load_act(kind, i):
+            rows = x_rows if kind == "x" else v_rows
+            width = D if kind == "x" else V
+            t = keep.tile([P, width], BF16, name="raw_%s%d" % (kind, i), align_bytes=64)
+            nc.sync.dma_start(out=t[:], in_=rows[:, i, :])
+            raw[kind, i] = t
+
+        def clear_plane(c0, c1):
+            t = keep.tile([P, X_PASSES, (c1 - c0) * NC], U8, name="w_plane%d" % c0, align_bytes=64)
+            nc.vector.memset(t[:].rearrange("p g n -> p (g n)").bitcast(I32), 0)
+            for c in range(c0, c1):
+                w_planes[c] = (t, c0)
+
+        def load_plane(c0, c1):
+            t = w_planes[c0][0]
+            for q in range(4):
+                nc.sync.dma_start(
+                    out=t[32 * q : 32 * q + 4, :, :].bitcast(I32),
+                    in_=wf_scales[:, 4 * q : 4 * q + 4, c0 * NC : c1 * NC].rearrange("g r n -> r g n").bitcast(I32),
+                )
+
+        def load_w(g, c0, c1):
+            t = keep.tile([P, (c1 - c0) * 2 * NC], U8, name="w_words%d_%d" % (g, c0), align_bytes=64)
+            nc.sync.dma_start(out=t[:].bitcast(I32), in_=wf_words[g, :, c0 * 2 * NC : c1 * 2 * NC].bitcast(I32))
+            for c in range(c0, c1):
+                w_words[g, c] = t[:, (c - c0) * 2 * NC : (c - c0 + 1) * 2 * NC]
+
+        def load_wo(c, g):
+            t = keep.tile([P, 4, NC], BF16, name="wo_raw%d_%d" % (c, g), align_bytes=64)
+            nc.sync.dma_start(
+                out=t[:], in_=wo[g * 512 : (g + 1) * 512, c * NC : (c + 1) * NC].rearrange("(p j) n -> p j n", j=4)
+            )
+            wo_raw[c, g] = t
+
+        def parts(kind):
+            return [(0, 2), (2, 3)] if kind == "x" else [(0, 2)]
+
+        def scale(kind, i):
+            width = D if kind == "x" else V
+            t = work.tile([P, width], BF16, name="ordered_" + kind, align_bytes=64)
+            factor = share_x if kind == "x" else share_v
+            nc.vector.tensor_scalar(
+                out=t[:].rearrange("p (u q e) -> p u q e", u=2, e=2),
+                in0=raw[kind, i][:].rearrange("p (q u e) -> p u q e", u=2, e=2),
+                scalar1=factor[:, i : i + 1],
+                scalar2=None,
+                op0=ALU.mult,
+            )
+            ordered[kind, i] = t
+
+        def turn(kind, i):
+            words = ordered[kind, i][:].bitcast(F32)
+            half = words.shape[1] // 2
+            for g0, g1 in parts(kind):
+                b, bank = take_bank()
+                for g in range(g0, g1):
+                    for u in range(2):
+                        col = ((g - g0) * 2 + u) * P
+                        nc.tensor.transpose(
+                            bank[:, col : col + P], words[:, u * half + g * P : u * half + (g + 1) * P], ident[:]
+                        )
+                turned[kind, i, g0] = (b, bank)
+
+        def pair_up(dst_words, bank, n):
+            nc.scalar.copy(
+                out=dst_words.rearrange("p (g r u) -> p g r u", g=n, u=2),
+                in_=bank[:, : n * 2 * P].rearrange("p (g u r) -> p g r u", g=n, u=2),
+            )
+
+        def empty(kind, i):
+            for g0, g1 in parts(kind):
+                b, bank = turned[kind, i, g0]
+                t = work.tile([P, (g1 - g0) * 512], BF16, name="grouped%d" % (g1 - g0), align_bytes=64, bufs=4)
+                pair_up(t[:].bitcast(F32), bank, g1 - g0)
+                free_banks.append(b)
+                grouped[kind, i, g0] = t
+
+        def quantise(kind, i):
+            for g0, g1 in parts(kind):
+                cd = keep.tile([P, (g1 - g0) * P], U32, name="codes_%s%d_%d" % (kind, i, g0), align_bytes=64)
+                sc = keep.tile([P, (g1 - g0) * P], U8, name="plane_%s%d_%d" % (kind, i, g0), align_bytes=64)
+                nc.vector.quantize_mx(out=cd[:].bitcast(FP8X4), scales=sc[:], in_=grouped[kind, i, g0][:])
+                for g in range(g0, g1):
+                    cols = slice((g - g0) * P, (g - g0 + 1) * P)
+                    codes[kind, i, g] = (cd[:, cols], sc[:, cols])
+
+        def interleave(c, g, h, engine):
+            if h == 0:
+                wo_grouped[c, g] = work.tile([P, NC, 4], BF16, name="wo_grouped", align_bytes=64)
+            cols = slice(h * NC // 2, (h + 1) * NC // 2)
+            dst = wo_grouped[c, g][:, cols, :].rearrange("p (a i) t -> p a t i", i=4)
+            src = wo_raw[c, g][:, :, cols].rearrange("p t (a i) -> p a t i", i=4)
+            if engine == "s":
+                nc.scalar.copy(out=dst, in_=src)
+            else:
+                nc.vector.tensor_copy(out=dst, in_=src)
+
+        def quantise_wo(c, g):
+            cd = keep.tile([P, NC], U32, name="wo_codes%d_%d" % (c, g), align_bytes=64)
+            sc = keep.tile([P, NC], U8, name="wo_plane%d_%d" % (c, g), align_bytes=64)
+            nc.vector.quantize_mx(
+                out=cd[:].bitcast(FP8X4), scales=sc[:], in_=wo_grouped[c, g][:].rearrange("p n t -> p (n t)")
+            )
+            wo_codes[c, g] = (cd, sc)
+
+        def mul_x(i, c):
+            acc[i, c] = take_bank()
+            plane, c0 = w_planes[c]
+            for g in range(X_PASSES):
+                cd, sc = codes["x", i, g]
+                nc.tensor.matmul_mx(
+                    out=acc[i, c][1][:],
+                    lhsT=cd.bitcast(FP8X4),
+                    lhsT_scale=sc,
+                    rhs=w_words[g, c].bitcast(FP4X4),
+                    rhs_scale=plane[:, g, (c - c0) * NC : (c - c0 + 1) * NC],
+                    start=(g == 0),
+                    stop=False,
+                )
+
+        def mul_v(i, c):
+            for g in range(V_PASSES):
+                cd, sc = codes["v", i, g]
+                wc, ws = wo_codes[c, g]
+                nc.tensor.matmul_mx(
+                    out=acc[i, c][1][:],
+                    lhsT=cd.bitcast(FP8X4),
+                    lhsT_scale=sc,
+                    rhs=wc[:].bitcast(FP8X4),
+                    rhs_scale=ws[:],
+                    start=False,
+                    stop=(g == V_PASSES - 1),
+                )
+
+        def finish(i, c):
+            b, bank = acc[i, c]
+            t = keep.tile([P, NC], F32, name="res%d_%d" % (i, c))
+            nc.vector.tensor_tensor(out=t[:], in0=bank[:], in1=bias_rows[:, c * NC : (c + 1) * NC], op=ALU.add)
+            free_banks.append(b)
+            res[i, c] = t
+
+        def store(i, c):
+            nc.sync.dma_start(out=out_rows[:, i, c * NC : (c + 1) * NC], in_=res[i, c][:])
+
+        def spread_bias():
+            words = bias_sb[:].rearrange("p c e -> p (c e)").bitcast(F32)
+            for c0, c1 in parts("x"):
+                b, bank = take_bank()
+                for j in range(2 * c0, 2 * c1):
+                    col = (j - 2 * c0) * P
+                    nc.tensor.transpose(bank[:, col : col + P], words[:, j : j + 1].to_broadcast([P, P]), ident[:])
+                pair_up(bias_rows[:, c0 * NC : c1 * NC].bitcast(F32), bank, c1 - c0)
+                free_banks.append(b)
+
+        bias_sb = keep.tile([P, CHUNKS, 4], BF16)
+        nc.gpsimd.dma_start(out=bias_sb[:], in_=bias.rearrange("(c p e) -> p c e", p=P, e=4))
+        bias_rows = keep.tile([P, D], BF16, align_bytes=64)
+        ident = keep.tile([P, P], F32)
+        make_identity(nc, ident[:])
+        warm = keep.tile([P, 1], F32)
+        warm_out = keep.tile([P, 1], F32)
+        nc.vector.memset(warm[:], 0.0)
+        nc.scalar.activation(out=warm_out[:], in_=warm[:], func=ACT.Sigmoid)
+        mix_sb = keep.tile([P, TILES], BF16)
+        nc.sync.dma_start(out=mix_sb[:], in_=mix.rearrange("(p i) o -> p (i o)", i=TILES))
+        share_x = keep.tile([P, TILES], F32)
+        share_v = keep.tile([P, TILES], F32)
+        nc.scalar.activation(out=share_x[:], in_=mix_sb[:], func=ACT.Sigmoid, scale=-1.0)
+        nc.scalar.activation(out=share_v[:], in_=mix_sb[:], func=ACT.Sigmoid)
+
+        def prep(kind, i):
+            scale(kind, i)
+            turn(kind, i)
+            empty(kind, i)
+            quantise(kind, i)
+
+        def prep_wo(c, engines):
+            for g in range(V_PASSES):
+                for h in range(2):
+                    interleave(c, g, h, engines[2 * g + h])
+                quantise_wo(c, g)
+
+        def close(i, c):
+            mul_v(i, c)
+            finish(i, c)
+
+        clear_plane(0, 2)
+        clear_plane(2, 3)
+        load_act("x", 0)
+        load_act("x", 1)
+        load_plane(0, 2)
+        for g in range(X_PASSES):
+            load_w(g, 0, 2)
+        load_act("x", 2)
+        load_wo(0, 0)
+        load_act("v", 0)
+        load_wo(0, 1)
+        load_act("v", 1)
+        load_act("v", 2)
+        load_wo(1, 0)
+        load_wo(1, 1)
+        for i in range(3, 6):
+            load_act("x", i)
+            load_act("v", i)
+        load_plane(2, 3)
+        load_wo(2, 0)
+        load_wo(2, 1)
+        for i in range(6, 8):
+            load_act("x", i)
+            load_act("v", i)
+        for g in range(X_PASSES):
+            load_w(g, 2, 3)
+
+        prep("x", 0)
+        prep("x", 1)
+        spread_bias()
+        mul_x(0, 0)
+        mul_x(0, 1)
+        prep("x", 2)
+        mul_x(1, 0)
+        mul_x(1, 1)
+        prep("v", 0)
+        prep_wo(0, "sssv")
+        mul_x(2, 0)
+        mul_x(2, 1)
+        prep("v", 1)
+        close(0, 0)
+        prep("v", 2)
+        close(1, 0)
+        prep("x", 3)
+        prep_wo(1, "sssv")
+        close(2, 0)
+        mul_x(3, 0)
+        prep("v", 3)
+        close(0, 1)
+        close(1, 1)
+        prep("x", 4)
+        close(2, 1)
+        close(3, 0)
+        prep("v", 4)
+        mul_x(3, 1)
+        close(3, 1)
+        for i in range(4):
+            for c in range(2):
+                store(i, c)
+        for i in range(4, TILES):
+            mul_x(i, 0)
+            close(i, 0)
+            store(i, 0)
+            if i < TILES - 1:
+                prep("x", i + 1)
+                prep("v", i + 1)
+            if i == 5:
+                prep_wo(2, "ssss")
+            mul_x(i, 1)
+            close(i, 1)
+            store(i, 1)
+        for i in range(TILES):
+            mul_x(i, 2)
+            close(i, 2)
+            store(i, 2)

@@ -35,7 +35,7 @@ def tile_value_residual_projection_s1_kernel(tc, v1, x, mix, wo, wf_words, wf_sc
         keep = ctx.enter_context(tc.tile_pool(name="keep", bufs=1))
         work = ctx.enter_context(tc.tile_pool(name="work", bufs=3))
         psum = ctx.enter_context(tc.psum_pool(name="psum", bufs=1))
-        ctx.enter_context(tc.manual_schedule(engines={ENG.PE, ENG.SP}))
+        ctx.enter_context(tc.manual_schedule())
 
         free_banks = list(range(8))
         raw = {}
@@ -73,8 +73,8 @@ def tile_value_residual_projection_s1_kernel(tc, v1, x, mix, wo, wf_words, wf_sc
             t = w_planes[c0][0]
             for q in range(4):
                 nc.sync.dma_start(
-                    out=t[32 * q : 32 * q + 4, :, :].bitcast(I32),
-                    in_=wf_scales[:, 4 * q : 4 * q + 4, c0 * NC : c1 * NC].rearrange("g r n -> r g n").bitcast(I32),
+                    out=t[q:P:32, :, :].bitcast(I32),
+                    in_=wf_scales[:, q:16:4, c0 * NC : c1 * NC].rearrange("g r n -> r g n").bitcast(I32),
                 )
 
         def load_w(g, c0, c1):
@@ -200,6 +200,43 @@ def tile_value_residual_projection_s1_kernel(tc, v1, x, mix, wo, wf_words, wf_sc
         def store(i, c):
             nc.sync.dma_start(out=out_rows[:, i, c * NC : (c + 1) * NC], in_=res[i, c][:])
 
+        def last_group(i, c):
+            plane, c0 = w_planes[c]
+            pieces = []
+            for n0, n1 in ((0, NC - P), (NC - P, NC)):
+                b, bank = take_bank()
+                for n in range(n0, n1, P):
+                    dst = bank[:, n - n0 : n - n0 + P]
+                    for g in range(X_PASSES):
+                        cd, sc = codes["x", i, g]
+                        nc.tensor.matmul_mx(
+                            out=dst,
+                            lhsT=cd.bitcast(FP8X4),
+                            lhsT_scale=sc,
+                            rhs=w_words[g, c][:, 2 * n : 2 * (n + P)].bitcast(FP4X4),
+                            rhs_scale=plane[:, g, (c - c0) * NC + n : (c - c0) * NC + n + P],
+                            start=(g == 0),
+                            stop=False,
+                        )
+                    for g in range(V_PASSES):
+                        cd, sc = codes["v", i, g]
+                        wc, ws = wo_codes[c, g]
+                        nc.tensor.matmul_mx(
+                            out=dst,
+                            lhsT=cd.bitcast(FP8X4),
+                            lhsT_scale=sc,
+                            rhs=wc[:, n : n + P].bitcast(FP8X4),
+                            rhs_scale=ws[:, n : n + P],
+                            start=False,
+                            stop=(g == V_PASSES - 1),
+                        )
+                pieces.append((n0, n1, bank))
+            for n0, n1, bank in pieces:
+                t = keep.tile([P, n1 - n0], F32, name="res_last%d" % n0)
+                cols = slice(c * NC + n0, c * NC + n1)
+                nc.vector.tensor_tensor(out=t[:], in0=bank[:, : n1 - n0], in1=bias_rows[:, cols], op=ALU.add)
+                nc.sync.dma_start(out=out_rows[:, i, cols], in_=t[:])
+
         def spread_bias():
             words = bias_sb[:].rearrange("p c e -> p (c e)").bitcast(F32)
             for c0, c1 in parts("x"):
@@ -211,7 +248,7 @@ def tile_value_residual_projection_s1_kernel(tc, v1, x, mix, wo, wf_words, wf_sc
                 free_banks.append(b)
 
         bias_sb = keep.tile([P, CHUNKS, 4], BF16)
-        nc.gpsimd.dma_start(out=bias_sb[:], in_=bias.rearrange("(c p e) -> p c e", p=P, e=4))
+        nc.scalar.dma_start(out=bias_sb[:], in_=bias.rearrange("(c p e) -> p c e", p=P, e=4))
         bias_rows = keep.tile([P, D], BF16, align_bytes=64)
         ident = keep.tile([P, P], F32)
         make_identity(nc, ident[:])
@@ -226,94 +263,211 @@ def tile_value_residual_projection_s1_kernel(tc, v1, x, mix, wo, wf_words, wf_sc
         nc.scalar.activation(out=share_x[:], in_=mix_sb[:], func=ACT.Sigmoid, scale=-1.0)
         nc.scalar.activation(out=share_v[:], in_=mix_sb[:], func=ACT.Sigmoid)
 
-        def prep(kind, i):
-            scale(kind, i)
-            turn(kind, i)
-            empty(kind, i)
-            quantise(kind, i)
-
-        def prep_wo(c, engines):
-            for g in range(V_PASSES):
-                for h in range(2):
-                    interleave(c, g, h, engines[2 * g + h])
-                quantise_wo(c, g)
-
-        def close(i, c):
-            mul_v(i, c)
-            finish(i, c)
-
         clear_plane(0, 2)
         clear_plane(2, 3)
         load_act("x", 0)
         load_act("x", 1)
         load_plane(0, 2)
-        for g in range(X_PASSES):
-            load_w(g, 0, 2)
+        load_w(0, 0, 2)
+        load_w(1, 0, 2)
+        load_w(2, 0, 2)
         load_act("x", 2)
         load_wo(0, 0)
         load_act("v", 0)
         load_wo(0, 1)
         load_act("v", 1)
         load_act("v", 2)
+        load_act("x", 3)
         load_wo(1, 0)
         load_wo(1, 1)
-        for i in range(3, 6):
-            load_act("x", i)
-            load_act("v", i)
+        load_act("v", 3)
+        load_act("x", 4)
+        load_act("v", 4)
+        load_act("x", 5)
+        load_act("v", 5)
+        load_act("x", 6)
+        load_act("v", 6)
         load_plane(2, 3)
         load_wo(2, 0)
         load_wo(2, 1)
-        for i in range(6, 8):
-            load_act("x", i)
-            load_act("v", i)
-        for g in range(X_PASSES):
-            load_w(g, 2, 3)
-
-        prep("x", 0)
-        prep("x", 1)
+        load_act("x", 7)
+        load_act("v", 7)
+        load_w(0, 2, 3)
+        load_w(1, 2, 3)
+        load_w(2, 2, 3)
         spread_bias()
+        scale("x", 0)
+        scale("x", 1)
+        turn("x", 0)
+        turn("x", 1)
+        empty("x", 0)
+        empty("x", 1)
+        quantise("x", 0)
+        quantise("x", 1)
         mul_x(0, 0)
         mul_x(0, 1)
-        prep("x", 2)
+        scale("x", 2)
+        turn("x", 2)
+        empty("x", 2)
         mul_x(1, 0)
         mul_x(1, 1)
-        prep("v", 0)
-        prep_wo(0, "sssv")
+        interleave(0, 0, 0, "v")
+        interleave(0, 0, 1, "v")
+        scale("v", 0)
+        turn("v", 0)
+        quantise("x", 2)
+        interleave(0, 1, 0, "s")
+        empty("v", 0)
+        interleave(0, 1, 1, "s")
+        quantise_wo(0, 0)
         mul_x(2, 0)
+        scale("v", 1)
+        scale("v", 2)
+        turn("v", 1)
+        turn("v", 2)
+        empty("v", 1)
+        empty("v", 2)
+        quantise("v", 0)
+        scale("x", 3)
+        quantise_wo(0, 1)
         mul_x(2, 1)
-        prep("v", 1)
-        close(0, 0)
-        prep("v", 2)
-        close(1, 0)
-        prep("x", 3)
-        prep_wo(1, "sssv")
-        close(2, 0)
+        turn("x", 3)
+        empty("x", 3)
+        quantise("v", 1)
+        quantise("v", 2)
+        mul_v(0, 0)
+        mul_v(1, 0)
+        mul_v(2, 0)
+        interleave(1, 0, 0, "s")
+        interleave(1, 0, 1, "s")
+        interleave(1, 1, 0, "v")
+        quantise("x", 3)
+        scale("v", 3)
+        finish(0, 0)
         mul_x(3, 0)
-        prep("v", 3)
-        close(0, 1)
-        close(1, 1)
-        prep("x", 4)
-        close(2, 1)
-        close(3, 0)
-        prep("v", 4)
+        turn("v", 3)
+        empty("v", 3)
+        interleave(1, 1, 1, "v")
+        quantise_wo(1, 0)
         mul_x(3, 1)
-        close(3, 1)
-        for i in range(4):
-            for c in range(2):
-                store(i, c)
-        for i in range(4, TILES):
-            mul_x(i, 0)
-            close(i, 0)
-            store(i, 0)
-            if i < TILES - 1:
-                prep("x", i + 1)
-                prep("v", i + 1)
-            if i == 5:
-                prep_wo(2, "ssss")
-            mul_x(i, 1)
-            close(i, 1)
-            store(i, 1)
-        for i in range(TILES):
-            mul_x(i, 2)
-            close(i, 2)
-            store(i, 2)
+        quantise_wo(1, 1)
+        mul_v(0, 1)
+        mul_v(1, 1)
+        mul_v(2, 1)
+        finish(1, 0)
+        scale("x", 4)
+        finish(2, 0)
+        scale("v", 4)
+        turn("x", 4)
+        turn("v", 4)
+        empty("x", 4)
+        empty("v", 4)
+        quantise("v", 3)
+        mul_v(3, 0)
+        mul_v(3, 1)
+        finish(0, 1)
+        quantise("x", 4)
+        quantise("v", 4)
+        scale("x", 5)
+        scale("v", 5)
+        finish(1, 1)
+        finish(2, 1)
+        mul_x(4, 0)
+        mul_v(4, 0)
+        turn("x", 5)
+        turn("v", 5)
+        empty("x", 5)
+        empty("v", 5)
+        interleave(2, 0, 0, "s")
+        interleave(2, 0, 1, "s")
+        mul_x(4, 1)
+        mul_v(4, 1)
+        finish(3, 0)
+        quantise("x", 5)
+        quantise("v", 5)
+        scale("x", 6)
+        scale("v", 6)
+        finish(3, 1)
+        finish(4, 0)
+        finish(4, 1)
+        store(0, 0)
+        store(0, 1)
+        store(1, 0)
+        store(1, 1)
+        store(2, 0)
+        store(2, 1)
+        store(3, 0)
+        store(3, 1)
+        store(4, 0)
+        store(4, 1)
+        mul_x(5, 0)
+        mul_v(5, 0)
+        turn("x", 6)
+        turn("v", 6)
+        empty("x", 6)
+        empty("v", 6)
+        interleave(2, 1, 0, "s")
+        interleave(2, 1, 1, "s")
+        finish(5, 0)
+        store(5, 0)
+        mul_x(5, 1)
+        mul_v(5, 1)
+        quantise("x", 6)
+        quantise("v", 6)
+        finish(5, 1)
+        store(5, 1)
+        scale("x", 7)
+        scale("v", 7)
+        mul_x(6, 0)
+        mul_v(6, 0)
+        turn("x", 7)
+        turn("v", 7)
+        empty("x", 7)
+        empty("v", 7)
+        finish(6, 0)
+        store(6, 0)
+        mul_x(6, 1)
+        mul_v(6, 1)
+        quantise("x", 7)
+        quantise("v", 7)
+        finish(6, 1)
+        store(6, 1)
+        quantise_wo(2, 0)
+        quantise_wo(2, 1)
+        mul_x(7, 0)
+        mul_v(7, 0)
+        finish(7, 0)
+        store(7, 0)
+        mul_x(7, 1)
+        mul_v(7, 1)
+        finish(7, 1)
+        store(7, 1)
+        mul_x(0, 2)
+        mul_v(0, 2)
+        finish(0, 2)
+        store(0, 2)
+        mul_x(1, 2)
+        mul_v(1, 2)
+        finish(1, 2)
+        store(1, 2)
+        mul_x(2, 2)
+        mul_v(2, 2)
+        finish(2, 2)
+        store(2, 2)
+        mul_x(3, 2)
+        mul_v(3, 2)
+        finish(3, 2)
+        store(3, 2)
+        mul_x(4, 2)
+        mul_v(4, 2)
+        finish(4, 2)
+        store(4, 2)
+        mul_x(5, 2)
+        mul_v(5, 2)
+        finish(5, 2)
+        store(5, 2)
+        mul_x(6, 2)
+        mul_v(6, 2)
+        finish(6, 2)
+        store(6, 2)
+        last_group(7, 2)

@@ -203,7 +203,7 @@ def tile_value_residual_projection_s1_kernel(tc, v1, x, mix, wo, wf_words, wf_sc
         def last_group(i, c):
             plane, c0 = w_planes[c]
             pieces = []
-            for n0, n1 in ((0, NC - P), (NC - P, NC)):
+            for n0, n1 in ((0, NC - 2 * P), (NC - 2 * P, NC - P), (NC - P, NC)):
                 b, bank = take_bank()
                 for n in range(n0, n1, P):
                     dst = bank[:, n - n0 : n - n0 + P]
@@ -278,20 +278,20 @@ def tile_value_residual_projection_s1_kernel(tc, v1, x, mix, wo, wf_words, wf_sc
         load_act("v", 1)
         load_act("v", 2)
         load_act("x", 3)
-        load_wo(1, 0)
-        load_wo(1, 1)
         load_act("v", 3)
         load_act("x", 4)
+        load_wo(1, 0)
         load_act("v", 4)
+        load_wo(1, 1)
         load_act("x", 5)
         load_act("v", 5)
         load_act("x", 6)
         load_act("v", 6)
+        load_act("x", 7)
+        load_act("v", 7)
         load_plane(2, 3)
         load_wo(2, 0)
         load_wo(2, 1)
-        load_act("x", 7)
-        load_act("v", 7)
         load_w(0, 2, 3)
         load_w(1, 2, 3)
         load_w(2, 2, 3)
@@ -338,109 +338,109 @@ def tile_value_residual_projection_s1_kernel(tc, v1, x, mix, wo, wf_words, wf_sc
         mul_v(0, 0)
         mul_v(1, 0)
         mul_v(2, 0)
+        scale("v", 3)
+        quantise("x", 3)
+        scale("x", 4)
+        finish(0, 0)
+        finish(1, 0)
         interleave(1, 0, 0, "s")
         interleave(1, 0, 1, "s")
-        interleave(1, 1, 0, "v")
-        quantise("x", 3)
-        scale("v", 3)
-        finish(0, 0)
-        mul_x(3, 0)
         turn("v", 3)
+        turn("x", 4)
         empty("v", 3)
-        interleave(1, 1, 1, "v")
-        quantise_wo(1, 0)
+        empty("x", 4)
+        interleave(1, 1, 0, "s")
+        mul_x(3, 0)
         mul_x(3, 1)
+        finish(2, 0)
+        quantise("v", 3)
+        mul_v(3, 0)
+        scale("v", 4)
+        scale("x", 5)
+        quantise("x", 4)
+        finish(3, 0)
+        turn("v", 4)
+        turn("x", 5)
+        empty("v", 4)
+        empty("x", 5)
+        quantise_wo(1, 0)
+        interleave(1, 1, 1, "v")
+        mul_x(4, 0)
+        mul_x(4, 1)
+        quantise("v", 4)
+        mul_v(4, 0)
         quantise_wo(1, 1)
         mul_v(0, 1)
         mul_v(1, 1)
         mul_v(2, 1)
-        finish(1, 0)
-        scale("x", 4)
-        finish(2, 0)
-        scale("v", 4)
-        turn("x", 4)
-        turn("v", 4)
-        empty("x", 4)
-        empty("v", 4)
-        quantise("v", 3)
-        mul_v(3, 0)
         mul_v(3, 1)
-        finish(0, 1)
-        quantise("x", 4)
-        quantise("v", 4)
-        scale("x", 5)
+        mul_v(4, 1)
+        quantise("x", 5)
         scale("v", 5)
-        finish(1, 1)
-        finish(2, 1)
-        mul_x(4, 0)
-        mul_v(4, 0)
-        turn("x", 5)
+        finish(4, 0)
+        scale("x", 6)
+        finish(0, 1)
         turn("v", 5)
-        empty("x", 5)
+        turn("x", 6)
         empty("v", 5)
+        empty("x", 6)
         interleave(2, 0, 0, "s")
         interleave(2, 0, 1, "s")
-        mul_x(4, 1)
-        mul_v(4, 1)
-        finish(3, 0)
-        quantise("x", 5)
-        quantise("v", 5)
-        scale("x", 6)
-        scale("v", 6)
-        finish(3, 1)
-        finish(4, 0)
-        finish(4, 1)
-        store(0, 0)
-        store(0, 1)
-        store(1, 0)
-        store(1, 1)
-        store(2, 0)
-        store(2, 1)
-        store(3, 0)
-        store(3, 1)
-        store(4, 0)
-        store(4, 1)
+        finish(1, 1)
         mul_x(5, 0)
-        mul_v(5, 0)
-        turn("x", 6)
-        turn("v", 6)
-        empty("x", 6)
-        empty("v", 6)
-        interleave(2, 1, 0, "s")
-        interleave(2, 1, 1, "s")
-        finish(5, 0)
-        store(5, 0)
         mul_x(5, 1)
+        finish(2, 1)
+        quantise("v", 5)
+        mul_v(5, 0)
         mul_v(5, 1)
         quantise("x", 6)
-        quantise("v", 6)
-        finish(5, 1)
-        store(5, 1)
+        scale("v", 6)
         scale("x", 7)
-        scale("v", 7)
-        mul_x(6, 0)
-        mul_v(6, 0)
+        finish(3, 1)
+        finish(4, 1)
+        turn("v", 6)
         turn("x", 7)
-        turn("v", 7)
+        empty("v", 6)
         empty("x", 7)
+        interleave(2, 1, 0, "s")
+        interleave(2, 1, 1, "s")
+        mul_x(6, 0)
+        finish(5, 0)
+        quantise("v", 6)
+        mul_x(6, 1)
+        mul_v(6, 0)
+        mul_v(6, 1)
+        finish(5, 1)
+        quantise("x", 7)
+        scale("v", 7)
+        quantise_wo(2, 0)
+        turn("v", 7)
         empty("v", 7)
         finish(6, 0)
-        store(6, 0)
-        mul_x(6, 1)
-        mul_v(6, 1)
-        quantise("x", 7)
-        quantise("v", 7)
-        finish(6, 1)
-        store(6, 1)
-        quantise_wo(2, 0)
-        quantise_wo(2, 1)
         mul_x(7, 0)
-        mul_v(7, 0)
-        finish(7, 0)
-        store(7, 0)
+        quantise("v", 7)
         mul_x(7, 1)
+        finish(6, 1)
+        quantise_wo(2, 1)
+        mul_v(7, 0)
         mul_v(7, 1)
+        finish(7, 0)
         finish(7, 1)
+        store(0, 0)
+        store(1, 0)
+        store(2, 0)
+        store(3, 0)
+        store(4, 0)
+        store(0, 1)
+        store(1, 1)
+        store(2, 1)
+        store(3, 1)
+        store(4, 1)
+        store(5, 0)
+        store(5, 1)
+        store(6, 0)
+        store(6, 1)
+        store(7, 0)
         store(7, 1)
         mul_x(0, 2)
         mul_v(0, 2)

from contextlib import ExitStack

import concourse.mybir as mybir
from concourse.masks import make_identity

M, V, D = 1024, 1024, 1536
FLOPS = 2 * M * (V + D) * D

F32 = mybir.dt.float32
BF16 = mybir.dt.bfloat16
I32 = mybir.dt.int32
U32 = mybir.dt.uint32
U8 = mybir.dt.uint8
FP8X4 = mybir.dt.float8_e4m3fn_x4
FP4X4 = mybir.dt.float4_e2m1fn_x4
ACT = mybir.ActivationFunctionType
ALU = mybir.AluOpType
ENG = mybir.EngineType

P = 128
TILES = M // P
NC = 512
CHUNKS = D // NC
X_PASSES = D // 512
V_PASSES = V // 512


def tile_value_residual_projection_s1_kernel(tc, v1, x, mix, wo, wf_words, wf_scales, bias, out):
    nc = tc.nc
    x_rows = x.rearrange("(p i) k -> p i k", i=TILES)
    v_rows = v1.rearrange("(p i) k -> p i k", i=TILES)
    out_rows = out.rearrange("(p i) n -> p i n", i=TILES)

    with ExitStack() as ctx:
        keep = ctx.enter_context(tc.tile_pool(name="keep", bufs=1))
        work = ctx.enter_context(tc.tile_pool(name="work", bufs=3))
        psum = ctx.enter_context(tc.psum_pool(name="psum", bufs=1))
        ctx.enter_context(tc.manual_schedule())

        free_banks = list(range(8))
        raw = {}
        ordered = {}
        turned = {}
        grouped = {}
        codes = {}
        w_words = {}
        w_planes = {}
        wo_raw = {}
        wo_grouped = {}
        wo_codes = {}
        acc = {}
        res = {}

        def take_bank():
            b = free_banks.pop(0)
            bank = psum.tile([P, 512], F32, tag="bank%d" % b, name="bank%d" % b)
            return b, bank

        def load_act(kind, i):
            rows = x_rows if kind == "x" else v_rows
            width = D if kind == "x" else V
            t = keep.tile([P, width], BF16, name="raw_%s%d" % (kind, i), align_bytes=64)
            nc.sync.dma_start(out=t[:], in_=rows[:, i, :])
            raw[kind, i] = t

        def clear_plane(c0, c1):
            t = keep.tile([P, X_PASSES, (c1 - c0) * NC], U8, name="w_plane%d" % c0, align_bytes=64)
            nc.vector.memset(t[:].rearrange("p g n -> p (g n)").bitcast(I32), 0)
            for c in range(c0, c1):
                w_planes[c] = (t, c0)

        def load_plane(c0, c1):
            t = w_planes[c0][0]
            for q in range(4):
                nc.sync.dma_start(
                    out=t[q:P:32, :, :].bitcast(I32),
                    in_=wf_scales[:, q:16:4, c0 * NC : c1 * NC].rearrange("g r n -> r g n").bitcast(I32),
                )

        def load_w(g, c0, c1):
            t = keep.tile([P, (c1 - c0) * 2 * NC], U8, name="w_words%d_%d" % (g, c0), align_bytes=64)
            nc.sync.dma_start(out=t[:].bitcast(I32), in_=wf_words[g, :, c0 * 2 * NC : c1 * 2 * NC].bitcast(I32))
            for c in range(c0, c1):
                w_words[g, c] = t[:, (c - c0) * 2 * NC : (c - c0 + 1) * 2 * NC]

        def load_wo(c, g):
            t = keep.tile([P, 4, NC], BF16, name="wo_raw%d_%d" % (c, g), align_bytes=64)
            nc.sync.dma_start(
                out=t[:], in_=wo[g * 512 : (g + 1) * 512, c * NC : (c + 1) * NC].rearrange("(p j) n -> p j n", j=4)
            )
            wo_raw[c, g] = t

        def parts(kind):
            return [(0, 2), (2, 3)] if kind == "x" else [(0, 2)]

        def scale(kind, i):
            width = D if kind == "x" else V
            t = work.tile([P, width], BF16, name="ordered_" + kind, align_bytes=64)
            factor = share_x if kind == "x" else share_v
            nc.vector.tensor_scalar(
                out=t[:].rearrange("p (u q e) -> p u q e", u=2, e=2),
                in0=raw[kind, i][:].rearrange("p (q u e) -> p u q e", u=2, e=2),
                scalar1=factor[:, i : i + 1],
                scalar2=None,
                op0=ALU.mult,
            )
            ordered[kind, i] = t

        def turn(kind, i):
            words = ordered[kind, i][:].bitcast(F32)
            half = words.shape[1] // 2
            for g0, g1 in parts(kind):
                b, bank = take_bank()
                for g in range(g0, g1):
                    for u in range(2):
                        col = ((g - g0) * 2 + u) * P
                        nc.tensor.transpose(
                            bank[:, col : col + P], words[:, u * half + g * P : u * half + (g + 1) * P], ident[:]
                        )
                turned[kind, i, g0] = (b, bank)

        def pair_up(dst_words, bank, n):
            nc.scalar.copy(
                out=dst_words.rearrange("p (g r u) -> p g r u", g=n, u=2),
                in_=bank[:, : n * 2 * P].rearrange("p (g u r) -> p g r u", g=n, u=2),
            )

        def empty(kind, i):
            for g0, g1 in parts(kind):
                b, bank = turned[kind, i, g0]
                t = work.tile([P, (g1 - g0) * 512], BF16, name="grouped%d" % (g1 - g0), align_bytes=64, bufs=4)
                pair_up(t[:].bitcast(F32), bank, g1 - g0)
                free_banks.append(b)
                grouped[kind, i, g0] = t

        def quantise(kind, i):
            for g0, g1 in parts(kind):
                cd = keep.tile([P, (g1 - g0) * P], U32, name="codes_%s%d_%d" % (kind, i, g0), align_bytes=64)
                sc = keep.tile([P, (g1 - g0) * P], U8, name="plane_%s%d_%d" % (kind, i, g0), align_bytes=64)
                nc.vector.quantize_mx(out=cd[:].bitcast(FP8X4), scales=sc[:], in_=grouped[kind, i, g0][:])
                for g in range(g0, g1):
                    cols = slice((g - g0) * P, (g - g0 + 1) * P)
                    codes[kind, i, g] = (cd[:, cols], sc[:, cols])

        def interleave(c, g, h, engine):
            if h == 0:
                wo_grouped[c, g] = work.tile([P, NC, 4], BF16, name="wo_grouped", align_bytes=64)
            cols = slice(h * NC // 2, (h + 1) * NC // 2)
            dst = wo_grouped[c, g][:, cols, :].rearrange("p (a i) t -> p a t i", i=4)
            src = wo_raw[c, g][:, :, cols].rearrange("p t (a i) -> p a t i", i=4)
            if engine == "s":
                nc.scalar.copy(out=dst, in_=src)
            else:
                nc.vector.tensor_copy(out=dst, in_=src)

        def quantise_wo(c, g):
            cd = keep.tile([P, NC], U32, name="wo_codes%d_%d" % (c, g), align_bytes=64)
            sc = keep.tile([P, NC], U8, name="wo_plane%d_%d" % (c, g), align_bytes=64)
            nc.vector.quantize_mx(
                out=cd[:].bitcast(FP8X4), scales=sc[:], in_=wo_grouped[c, g][:].rearrange("p n t -> p (n t)")
            )
            wo_codes[c, g] = (cd, sc)

        def mul_x(i, c):
            acc[i, c] = take_bank()
            plane, c0 = w_planes[c]
            for g in range(X_PASSES):
                cd, sc = codes["x", i, g]
                nc.tensor.matmul_mx(
                    out=acc[i, c][1][:],
                    lhsT=cd.bitcast(FP8X4),
                    lhsT_scale=sc,
                    rhs=w_words[g, c].bitcast(FP4X4),
                    rhs_scale=plane[:, g, (c - c0) * NC : (c - c0 + 1) * NC],
                    start=(g == 0),
                    stop=False,
                )

        def mul_v(i, c):
            for g in range(V_PASSES):
                cd, sc = codes["v", i, g]
                wc, ws = wo_codes[c, g]
                nc.tensor.matmul_mx(
                    out=acc[i, c][1][:],
                    lhsT=cd.bitcast(FP8X4),
                    lhsT_scale=sc,
                    rhs=wc[:].bitcast(FP8X4),
                    rhs_scale=ws[:],
                    start=False,
                    stop=(g == V_PASSES - 1),
                )

        def finish(i, c):
            b, bank = acc[i, c]
            t = keep.tile([P, NC], F32, name="res%d_%d" % (i, c))
            nc.vector.tensor_tensor(out=t[:], in0=bank[:], in1=bias_rows[:, c * NC : (c + 1) * NC], op=ALU.add)
            free_banks.append(b)
            res[i, c] = t

        def store(i, c):
            nc.sync.dma_start(out=out_rows[:, i, c * NC : (c + 1) * NC], in_=res[i, c][:])

        def last_group(i, c):
            plane, c0 = w_planes[c]
            pieces = []
            for n0, n1 in ((0, NC - 2 * P), (NC - 2 * P, NC - P), (NC - P, NC)):
                b, bank = take_bank()
                for n in range(n0, n1, P):
                    dst = bank[:, n - n0 : n - n0 + P]
                    for g in range(X_PASSES):
                        cd, sc = codes["x", i, g]
                        nc.tensor.matmul_mx(
                            out=dst,
                            lhsT=cd.bitcast(FP8X4),
                            lhsT_scale=sc,
                            rhs=w_words[g, c][:, 2 * n : 2 * (n + P)].bitcast(FP4X4),
                            rhs_scale=plane[:, g, (c - c0) * NC + n : (c - c0) * NC + n + P],
                            start=(g == 0),
                            stop=False,
                        )
                    for g in range(V_PASSES):
                        cd, sc = codes["v", i, g]
                        wc, ws = wo_codes[c, g]
                        nc.tensor.matmul_mx(
                            out=dst,
                            lhsT=cd.bitcast(FP8X4),
                            lhsT_scale=sc,
                            rhs=wc[:, n : n + P].bitcast(FP8X4),
                            rhs_scale=ws[:, n : n + P],
                            start=False,
                            stop=(g == V_PASSES - 1),
                        )
                pieces.append((n0, n1, bank))
            for n0, n1, bank in pieces:
                t = keep.tile([P, n1 - n0], F32, name="res_last%d" % n0)
                cols = slice(c * NC + n0, c * NC + n1)
                nc.vector.tensor_tensor(out=t[:], in0=bank[:, : n1 - n0], in1=bias_rows[:, cols], op=ALU.add)
                nc.sync.dma_start(out=out_rows[:, i, cols], in_=t[:])

        def spread_bias():
            words = bias_sb[:].rearrange("p c e -> p (c e)").bitcast(F32)
            for c0, c1 in parts("x"):
                b, bank = take_bank()
                for j in range(2 * c0, 2 * c1):
                    col = (j - 2 * c0) * P
                    nc.tensor.transpose(bank[:, col : col + P], words[:, j : j + 1].to_broadcast([P, P]), ident[:])
                pair_up(bias_rows[:, c0 * NC : c1 * NC].bitcast(F32), bank, c1 - c0)
                free_banks.append(b)

        bias_sb = keep.tile([P, CHUNKS, 4], BF16)
        nc.scalar.dma_start(out=bias_sb[:], in_=bias.rearrange("(c p e) -> p c e", p=P, e=4))
        bias_rows = keep.tile([P, D], BF16, align_bytes=64)
        ident = keep.tile([P, P], F32)
        make_identity(nc, ident[:])
        warm = keep.tile([P, 1], F32)
        warm_out = keep.tile([P, 1], F32)
        nc.vector.memset(warm[:], 0.0)
        nc.scalar.activation(out=warm_out[:], in_=warm[:], func=ACT.Sigmoid)
        mix_sb = keep.tile([P, TILES], BF16)
        nc.sync.dma_start(out=mix_sb[:], in_=mix.rearrange("(p i) o -> p (i o)", i=TILES))
        share_x = keep.tile([P, TILES], F32)
        share_v = keep.tile([P, TILES], F32)
        nc.scalar.activation(out=share_x[:], in_=mix_sb[:], func=ACT.Sigmoid, scale=-1.0)
        nc.scalar.activation(out=share_v[:], in_=mix_sb[:], func=ACT.Sigmoid)

        clear_plane(0, 2)
        clear_plane(2, 3)
        load_act("x", 0)
        load_act("x", 1)
        load_plane(0, 2)
        load_w(0, 0, 2)
        load_w(1, 0, 2)
        load_w(2, 0, 2)
        load_act("x", 2)
        load_wo(0, 0)
        load_act("v", 0)
        load_wo(0, 1)
        load_act("v", 1)
        load_act("v", 2)
        load_act("x", 3)
        load_act("v", 3)
        load_act("x", 4)
        load_wo(1, 0)
        load_act("v", 4)
        load_wo(1, 1)
        load_act("x", 5)
        load_act("v", 5)
        load_act("x", 6)
        load_act("v", 6)
        load_act("x", 7)
        load_act("v", 7)
        load_plane(2, 3)
        load_wo(2, 0)
        load_wo(2, 1)
        load_w(0, 2, 3)
        load_w(1, 2, 3)
        load_w(2, 2, 3)
        spread_bias()
        scale("x", 0)
        scale("x", 1)
        turn("x", 0)
        turn("x", 1)
        empty("x", 0)
        empty("x", 1)
        quantise("x", 0)
        quantise("x", 1)
        mul_x(0, 0)
        mul_x(0, 1)
        scale("x", 2)
        turn("x", 2)
        empty("x", 2)
        mul_x(1, 0)
        mul_x(1, 1)
        interleave(0, 0, 0, "v")
        interleave(0, 0, 1, "v")
        scale("v", 0)
        turn("v", 0)
        quantise("x", 2)
        interleave(0, 1, 0, "s")
        empty("v", 0)
        interleave(0, 1, 1, "s")
        quantise_wo(0, 0)
        mul_x(2, 0)
        scale("v", 1)
        scale("v", 2)
        turn("v", 1)
        turn("v", 2)
        empty("v", 1)
        empty("v", 2)
        quantise("v", 0)
        scale("x", 3)
        quantise_wo(0, 1)
        mul_x(2, 1)
        turn("x", 3)
        empty("x", 3)
        quantise("v", 1)
        quantise("v", 2)
        mul_v(0, 0)
        mul_v(1, 0)
        mul_v(2, 0)
        scale("v", 3)
        quantise("x", 3)
        scale("x", 4)
        finish(0, 0)
        finish(1, 0)
        interleave(1, 0, 0, "s")
        interleave(1, 0, 1, "s")
        turn("v", 3)
        turn("x", 4)
        empty("v", 3)
        empty("x", 4)
        interleave(1, 1, 0, "s")
        mul_x(3, 0)
        mul_x(3, 1)
        finish(2, 0)
        quantise("v", 3)
        mul_v(3, 0)
        scale("v", 4)
        scale("x", 5)
        quantise("x", 4)
        finish(3, 0)
        turn("v", 4)
        turn("x", 5)
        empty("v", 4)
        empty("x", 5)
        quantise_wo(1, 0)
        interleave(1, 1, 1, "v")
        mul_x(4, 0)
        mul_x(4, 1)
        quantise("v", 4)
        mul_v(4, 0)
        quantise_wo(1, 1)
        mul_v(0, 1)
        mul_v(1, 1)
        mul_v(2, 1)
        mul_v(3, 1)
        mul_v(4, 1)
        quantise("x", 5)
        scale("v", 5)
        finish(4, 0)
        scale("x", 6)
        finish(0, 1)
        turn("v", 5)
        turn("x", 6)
        empty("v", 5)
        empty("x", 6)
        interleave(2, 0, 0, "s")
        interleave(2, 0, 1, "s")
        finish(1, 1)
        mul_x(5, 0)
        mul_x(5, 1)
        finish(2, 1)
        quantise("v", 5)
        mul_v(5, 0)
        mul_v(5, 1)
        quantise("x", 6)
        scale("v", 6)
        scale("x", 7)
        finish(3, 1)
        finish(4, 1)
        turn("v", 6)
        turn("x", 7)
        empty("v", 6)
        empty("x", 7)
        interleave(2, 1, 0, "s")
        interleave(2, 1, 1, "s")
        mul_x(6, 0)
        finish(5, 0)
        quantise("v", 6)
        mul_x(6, 1)
        mul_v(6, 0)
        mul_v(6, 1)
        finish(5, 1)
        quantise("x", 7)
        scale("v", 7)
        quantise_wo(2, 0)
        turn("v", 7)
        empty("v", 7)
        finish(6, 0)
        mul_x(7, 0)
        quantise("v", 7)
        mul_x(7, 1)
        finish(6, 1)
        quantise_wo(2, 1)
        mul_v(7, 0)
        mul_v(7, 1)
        finish(7, 0)
        finish(7, 1)
        store(0, 0)
        store(1, 0)
        store(2, 0)
        store(3, 0)
        store(4, 0)
        store(0, 1)
        store(1, 1)
        store(2, 1)
        store(3, 1)
        store(4, 1)
        store(5, 0)
        store(5, 1)
        store(6, 0)
        store(6, 1)
        store(7, 0)
        store(7, 1)
        mul_x(0, 2)
        mul_v(0, 2)
        finish(0, 2)
        store(0, 2)
        mul_x(1, 2)
        mul_v(1, 2)
        finish(1, 2)
        store(1, 2)
        mul_x(2, 2)
        mul_v(2, 2)
        finish(2, 2)
        store(2, 2)
        mul_x(3, 2)
        mul_v(3, 2)
        finish(3, 2)
        store(3, 2)
        mul_x(4, 2)
        mul_v(4, 2)
        finish(4, 2)
        store(4, 2)
        mul_x(5, 2)
        mul_v(5, 2)
        finish(5, 2)
        store(5, 2)
        mul_x(6, 2)
        mul_v(6, 2)
        finish(6, 2)
        store(6, 2)
        last_group(7, 2)
